import numpy as np
import ml_dtypes


def mxq(x, axis, fmt="e4m3"):
    dtype, down = {"e4m3": (ml_dtypes.float8_e4m3fn, 7), "e5m2": (ml_dtypes.float8_e5m2, 14)}[fmt]
    v = np.moveaxis(np.asarray(x, np.float32).astype(ml_dtypes.bfloat16).astype(np.float64), axis, -1)
    blocks = v.reshape(v.shape[:-1] + (-1, 32))
    amax = np.abs(blocks).max(-1, keepdims=True)
    byte = np.maximum(np.where(amax > 0, np.frexp(amax)[1] - 1 + 127, 0) - down, 1)
    scale = np.exp2(byte - 127.0)
    codes = (blocks / scale).astype(np.float32).astype(dtype).astype(np.float64)
    return np.moveaxis((codes * scale).reshape(v.shape), -1, axis)


WIDE = False


def mx_kscale(k):
    if not WIDE:
        return np.ones(k)
    levels = np.array([10, -10, 5, -5, 0])
    if k % 512:
        return np.exp2(np.random.permutation(np.resize(levels, k // 32))).repeat(32)
    a = np.empty((k // 512, 16))
    for p in range(k // 512):
        a[p, :8] = np.random.permutation(np.resize(levels, 8))
        for g in range(8):
            far = levels[np.abs(levels - a[p, g]) >= 10]
            a[p, g + 8] = far[np.random.randint(len(far))]
    return np.exp2(a.ravel()).repeat(32)


def f64(x):
    return np.asarray(x).astype(np.float64)


def striped8(idx):
    return np.asarray(idx).reshape(8, -1, 16).transpose(0, 2, 1).reshape(128, -1).astype(np.uint16)


def unstriped8(offs):
    return offs.reshape(8, 16, -1).transpose(0, 2, 1).reshape(8, -1).astype(np.int64)


def pick8(x, idx, run):
    r = np.arange(len(x))
    return x[r[:, None], idx[r % (8 * run) // run]]


E2M1 = np.array([0.0, 0.5, 1.0, 1.5, 2.0, 3.0, 4.0, 6.0, -0.0, -0.5, -1.0, -1.5, -2.0, -3.0, -4.0, -6.0])


def pack_weight(w, fmt):
    k, n = w.shape
    w = f64(np.asarray(w, np.float32).astype(ml_dtypes.bfloat16)).reshape(k // 32, 32, n)
    amax = np.abs(w).max(1)
    if fmt == "e4m3":
        byte = np.frexp(amax)[1] - 1 + 127 - 7
    else:
        mant, ex = np.frexp(amax / 6.0)
        byte = np.where(mant > 0.5, ex, ex - 1) + 127
    byte = np.clip(np.where(amax > 0, byte, 1), 1, 254)
    scaled = (w * np.exp2(127.0 - byte)[:, None, :]).reshape(k, n).astype(np.float32)
    by_word = np.ascontiguousarray(scaled.reshape(k // 512, 128, 4, n).transpose(0, 1, 3, 2))
    if fmt == "e4m3":
        words = by_word.astype(ml_dtypes.float8_e4m3fn).view(np.uint8)
    else:
        c = by_word.astype(ml_dtypes.float4_e2m1fn).view(np.uint8) & 0xF
        words = (c[..., 0::2] | (c[..., 1::2] << 4)).reshape(k // 512, 128, 2 * n)
    return np.ascontiguousarray(words), np.ascontiguousarray(byte.astype(np.uint8).reshape(k // 512, 16, n))


def unpack_weight(words, scales, fmt):
    g, _, n = scales.shape
    words = np.ascontiguousarray(words).reshape(g, 128, n, -1)
    if fmt == "e4m3":
        vals = words.view(ml_dtypes.float8_e4m3fn).astype(np.float64)
    else:
        nib = np.empty((g, 128, n, 4), np.uint8)
        nib[..., 0::2] = words & 0xF
        nib[..., 1::2] = words >> 4
        vals = E2M1[nib]
    vals = vals * np.repeat(np.exp2(scales.astype(np.float64) - 127.0), 8, axis=1)[..., None]
    return vals.transpose(0, 1, 3, 2).reshape(g * 512, n)


D, T, I, Q, G = 512, 1024, 512, 128, 64


def setup_inputs():
    n = np.random.standard_normal
    idx = np.stack([np.random.permutation(T)[:I] for _ in range(8)])
    idx2 = np.stack([np.random.permutation(T)[:I] for _ in range(8)])
    idx3 = np.stack([np.random.permutation(T)[:I] for _ in range(8)])
    idx4 = np.stack([np.random.permutation(T)[:I] for _ in range(8)])
    fd = mx_kscale(D)
    keysp = pack_weight(n((D, T)) / fd[:, None], "e2m1")
    return {
        "query": (n((D, Q)) * 1.0 / np.sqrt(D) * fd[:, None]).astype(np.float32),
        "keys_words": keysp[0],
        "keys_scales": keysp[1],
        "lam": (np.random.uniform(0.4, 1.0, (Q, 1))).astype(np.float32),
        "old": (np.random.uniform(0.0, 2.0, (Q, T))).astype(np.float32),
        "gainm": (np.random.uniform(0.5, 1.5, (Q, I))).astype(np.float32),
        "offs": striped8(idx),
        "offs2": striped8(idx2),
        "offs3": striped8(idx3),
        "offs4": striped8(idx4),
    }


def reference(query, keys_words, keys_scales, lam, old, gainm, offs, offs2, offs3, offs4):
    idx = unstriped8(offs)
    idx2 = unstriped8(offs2)
    idx3 = unstriped8(offs3)
    idx4 = unstriped8(offs4)
    keysu = unpack_weight(keys_words, keys_scales, "e2m1")
    queryq = mxq(f64(query), 0, "e4m3")
    a = queryq.T @ keysu
    s = pick8(a, idx, 16) + np.tanh(pick8(a, idx2, 16) - pick8(a, idx3, 16)) * f64(lam)
    p = np.exp(s)
    pg = p.reshape(Q, G, I // G).sum(axis=2)
    z0 = np.sum(pg, axis=1, keepdims=True)
    k0 = 1.0 / (z0 - pg)
    kr = np.repeat(k0, I // G, axis=1)
    w = p * kr
    ws = w * f64(gainm) * 64.0
    wf = np.zeros((Q, T))
    wf[np.arange(Q)[:, None], idx4[np.arange(Q) % 128 // 16]] = ws
    y = f64(old) + wf
    return y

@@ -1,0 +1,193 @@
+from contextlib import ExitStack
+
+import concourse.mybir as mybir
+
+F32 = mybir.dt.float32
+BF16 = mybir.dt.bfloat16
+I32 = mybir.dt.int32
+U32 = mybir.dt.uint32
+U16 = mybir.dt.uint16
+U8 = mybir.dt.uint8
+FP8X4 = mybir.dt.float8_e4m3fn_x4
+FP4X4 = mybir.dt.float4_e2m1fn_x4
+ALU = mybir.AluOpType
+ACT = mybir.ActivationFunctionType
+AXIS = mybir.AxisListType
+
+P = 128
+D, T, I, Q, G = 512, 1024, 512, 128, 64
+RUN = I // G
+PACK = 4
+PASS_WIDTHS = (256, 256, 256, 128, 128)
+HALF = I // 2
+LIST_COLS = I // 16
+OUT_TILE = 256
+
+FLOPS = 2 * D * Q * T
+
+
+def tile_attend_seconded_outside_moved_heads_kernel(
+    tc, query, keys_words, keys_scales, lam, old, gainm, offs, offs2, offs3, offs4, out
+):
+    nc = tc.nc
+    with ExitStack() as ctx:
+        sb = ctx.enter_context(tc.tile_pool(name="sb", bufs=1))
+        ps = ctx.enter_context(tc.psum_pool(name="ps", bufs=1))
+
+        k_scales = sb.tile([P, T], U8, name="k_scales", align_bytes=64)
+        nc.vector.memset(k_scales[:].bitcast(I32), 0)
+        placed = sb.tile([P, T], F32, name="placed")
+        nc.vector.memset(placed[:], 0.0)
+
+        q_raw = sb.tile([P, PACK, Q], F32, name="q_raw")
+        nc.sync.dma_start(out=q_raw[:], in_=query.rearrange("(p j) q -> p j q", j=PACK))
+        scale_words = keys_scales[0].bitcast(I32)
+        for quad in range(4):
+            nc.sync.dma_start(
+                out=k_scales[32 * quad : 32 * quad + 4, :].bitcast(I32),
+                in_=scale_words[4 * quad : 4 * quad + 4, :],
+            )
+        k_words = sb.tile([P, 2 * T], U8, name="k_words", align_bytes=64)
+        nc.sync.dma_start(out=k_words[:].bitcast(I32), in_=keys_words[0].bitcast(I32))
+
+        opponent_list = sb.tile([P, LIST_COLS], U16, name="opponent_list")
+        nc.sync.dma_start(opponent_list[:], offs3)
+        own_list = sb.tile([P, LIST_COLS], U16, name="own_list")
+        nc.sync.dma_start(own_list[:], offs)
+        seconder_list = sb.tile([P, LIST_COLS], U16, name="seconder_list")
+        nc.sync.dma_start(seconder_list[:], offs2)
+        place_list = sb.tile([P, LIST_COLS], U16, name="place_list")
+        nc.sync.dma_start(place_list[:], offs4)
+
+        lam_sb = sb.tile([P, 1], F32, name="lam_sb")
+        nc.gpsimd.dma_start(out=lam_sb[:], in_=lam)
+        gain = sb.tile([P, I], F32, name="gain")
+        nc.gpsimd.dma_start(out=gain[:], in_=gainm)
+        old_sb = sb.tile([P, T], F32, name="old_sb")
+        nc.gpsimd.dma_start(out=old_sb[:], in_=old)
+
+        q_grouped = sb.tile([P, Q, PACK], BF16, name="q_grouped", align_bytes=64)
+        nc.vector.tensor_copy(out=q_grouped[:], in_=q_raw[:].rearrange("p j q -> p q j"))
+        q_codes = sb.tile([P, Q], U32, name="q_codes", align_bytes=64)
+        q_scales = sb.tile([P, Q], U8, name="q_scales", align_bytes=64)
+        nc.vector.quantize_mx(
+            out=q_codes[:].bitcast(FP8X4),
+            scales=q_scales[:],
+            in_=q_grouped[:].rearrange("p q j -> p (q j)"),
+        )
+
+        a = sb.tile([P, T], F32, name="a")
+        first = 0
+        for n, width in enumerate(PASS_WIDTHS):
+            cols = slice(first, first + width)
+            first = first + width
+            bank = ps.tile([P, width], F32, name="bank%d" % n)
+            nc.tensor.matmul_mx(
+                out=bank[:],
+                lhsT=q_codes[:].bitcast(FP8X4),
+                lhsT_scale=q_scales[:],
+                rhs=k_words[:, 2 * cols.start : 2 * cols.stop].bitcast(FP4X4),
+                rhs_scale=k_scales[:, cols],
+                start=True,
+                stop=True,
+            )
+            if n % 2 == 1:
+                nc.scalar.copy(out=a[:, cols], in_=bank[:])
+            else:
+                nc.vector.tensor_copy(out=a[:, cols], in_=bank[:])
+
+        halves = [slice(h * HALF, (h + 1) * HALF) for h in range(2)]
+        list_halves = [slice(h * LIST_COLS // 2, (h + 1) * LIST_COLS // 2) for h in range(2)]
+        group_halves = [slice(h * G // 2, (h + 1) * G // 2) for h in range(2)]
+
+        opponent = sb.tile([P, I], F32, name="opponent")
+        own = sb.tile([P, I], F32, name="own")
+        margin = sb.tile([P, I], F32, name="margin")
+        vote = sb.tile([P, I], F32, name="vote")
+        score = sb.tile([P, I], F32, name="score")
+        prob = sb.tile([P, I], F32, name="prob")
+        numer = sb.tile([P, I], F32, name="numer")
+        neg_max = sb.tile([P, 1], F32, name="neg_max")
+        half_sums = [sb.tile([P, 1], F32, name="half_sum%d" % h) for h in range(2)]
+        run_sums = sb.tile([P, G], F32, name="run_sums")
+        neg_outside = sb.tile([P, G], F32, name="neg_outside")
+        neg_recip = sb.tile([P, G], F32, name="neg_recip")
+        neg_recip_wide = [sb.tile([P, G // 2, RUN], F32, name="neg_recip_wide%d" % h) for h in range(2)]
+
+        for h in range(2):
+            nc.scalar.activation(opponent[:, halves[h]], a[:].indirect(opponent_list[:, list_halves[h]]), ACT.Copy)
+        nc.vector.tensor_copy(own[:, halves[0]], a[:].indirect(own_list[:, list_halves[0]]))
+        nc.scalar.activation(own[:, halves[1]], a[:].indirect(own_list[:, list_halves[1]]), ACT.Copy)
+        for h in range(2):
+            nc.vector.tensor_tensor(
+                margin[:, halves[h]], a[:].indirect(seconder_list[:, list_halves[h]]), opponent[:, halves[h]], ALU.subtract
+            )
+        for h in range(2):
+            nc.scalar.activation(vote[:, halves[h]], margin[:, halves[h]], ACT.Tanh)
+        nc.vector.tensor_reduce(out=neg_max[:], in_=own[:], axis=AXIS.X, op=ALU.max, negate=True)
+        for h in range(2):
+            nc.vector.scalar_tensor_tensor(
+                out=score[:, halves[h]], in0=vote[:, halves[h]], scalar=lam_sb[:], in1=own[:, halves[h]],
+                op0=ALU.mult, op1=ALU.add,
+            )
+        for h in range(2):
+            nc.scalar.activation(
+                prob[:, halves[h]], score[:, halves[h]], ACT.Exp, bias=neg_max[:], accum_out=half_sums[h][:]
+            )
+
+        def sum_runs(h):
+            nc.vector.tensor_reduce(
+                out=run_sums[:, group_halves[h]],
+                in_=prob[:, halves[h]].rearrange("p (g r) -> p g r", r=RUN),
+                axis=AXIS.X,
+                op=ALU.add,
+            )
+
+        def weigh(h):
+            nc.vector.scalar_tensor_tensor(
+                out=numer[:, halves[h]], in0=prob[:, halves[h]], scalar=-64.0, in1=gain[:, halves[h]],
+                op0=ALU.mult, op1=ALU.mult,
+            )
+
+        def outside(h):
+            nc.vector.tensor_scalar(
+                out=neg_outside[:, group_halves[h]], in0=run_sums[:, group_halves[h]],
+                scalar1=half_sums[0][:], scalar2=half_sums[1][:],
+                op0=ALU.subtract, op1=ALU.subtract,
+            )
+
+        def invert(h):
+            nc.vector.reciprocal(out=neg_recip[:, group_halves[h]], in_=neg_outside[:, group_halves[h]])
+
+        def spread(h, copy):
+            copy(
+                out=neg_recip_wide[h][:],
+                in_=neg_recip[:, group_halves[h]].unsqueeze(2).to_broadcast([P, G // 2, RUN]),
+            )
+
+        def place(h):
+            nc.vector.tensor_tensor(
+                placed[:].indirect(place_list[:, list_halves[h]]),
+                numer[:, halves[h]],
+                neg_recip_wide[h][:].rearrange("p g r -> p (g r)"),
+                ALU.mult,
+            )
+
+        sum_runs(0)
+        weigh(0)
+        outside(0)
+        sum_runs(1)
+        invert(0)
+        outside(1)
+        weigh(1)
+        spread(0, nc.vector.tensor_copy)
+        invert(1)
+        place(0)
+        spread(1, nc.scalar.copy)
+        place(1)
+
+        for n in range(T // OUT_TILE):
+            cols = slice(n * OUT_TILE, (n + 1) * OUT_TILE)
+            result = sb.tile([P, OUT_TILE], F32, name="result%d" % n)
+            nc.vector.tensor_tensor(result[:], placed[:, cols], old_sb[:, cols], ALU.add)
+            nc.sync.dma_start(out=out[:, cols], in_=result[:])

@@ -39,7 +39,7 @@ def tile_attend_seconded_outside_moved_heads_kernel(
         placed = sb.tile([P, T], F32, name="placed")
         nc.vector.memset(placed[:], 0.0)
 
-        q_raw = sb.tile([P, PACK, Q], F32, name="q_raw")
+        q_raw = sb.tile([P, PACK, Q], F32, name="q_raw", tag="query_then_gain")
         nc.sync.dma_start(out=q_raw[:], in_=query.rearrange("(p j) q -> p j q", j=PACK))
         scale_words = keys_scales[0].bitcast(I32)
         for quad in range(4):
@@ -60,14 +60,12 @@ def tile_attend_seconded_outside_moved_heads_kernel(
         nc.sync.dma_start(place_list[:], offs4)
 
         lam_sb = sb.tile([P, 1], F32, name="lam_sb")
-        nc.gpsimd.dma_start(out=lam_sb[:], in_=lam)
-        gain = sb.tile([P, I], F32, name="gain")
-        nc.gpsimd.dma_start(out=gain[:], in_=gainm)
-        old_sb = sb.tile([P, T], F32, name="old_sb")
-        nc.gpsimd.dma_start(out=old_sb[:], in_=old)
+        nc.sync.dma_start(out=lam_sb[:], in_=lam)
 
         q_grouped = sb.tile([P, Q, PACK], BF16, name="q_grouped", align_bytes=64)
         nc.vector.tensor_copy(out=q_grouped[:], in_=q_raw[:].rearrange("p j q -> p q j"))
+        gain = sb.tile([P, I], F32, name="gain", tag="query_then_gain")
+        nc.sync.dma_start(out=gain[:], in_=gainm)
         q_codes = sb.tile([P, Q], U32, name="q_codes", align_bytes=64)
         q_scales = sb.tile([P, Q], U8, name="q_scales", align_bytes=64)
         nc.vector.quantize_mx(
@@ -98,21 +96,21 @@ def tile_attend_seconded_outside_moved_heads_kernel(
 
         halves = [slice(h * HALF, (h + 1) * HALF) for h in range(2)]
         list_halves = [slice(h * LIST_COLS // 2, (h + 1) * LIST_COLS // 2) for h in range(2)]
-        group_halves = [slice(h * G // 2, (h + 1) * G // 2) for h in range(2)]
 
-        opponent = sb.tile([P, I], F32, name="opponent")
+        opponent = sb.tile([P, I], F32, name="opponent", tag="opponent_then_old")
         own = sb.tile([P, I], F32, name="own")
-        margin = sb.tile([P, I], F32, name="margin")
+        margin = sb.tile([P, I], F32, name="margin", tag="margin_then_old")
         vote = sb.tile([P, I], F32, name="vote")
         score = sb.tile([P, I], F32, name="score")
         prob = sb.tile([P, I], F32, name="prob")
         numer = sb.tile([P, I], F32, name="numer")
         neg_max = sb.tile([P, 1], F32, name="neg_max")
-        half_sums = [sb.tile([P, 1], F32, name="half_sum%d" % h) for h in range(2)]
+        piece_sums = [sb.tile([P, 1], F32, name="piece_sum%d" % c) for c in range(3)]
+        front_sum = sb.tile([P, 1], F32, name="front_sum")
         run_sums = sb.tile([P, G], F32, name="run_sums")
         neg_outside = sb.tile([P, G], F32, name="neg_outside")
         neg_recip = sb.tile([P, G], F32, name="neg_recip")
-        neg_recip_wide = [sb.tile([P, G // 2, RUN], F32, name="neg_recip_wide%d" % h) for h in range(2)]
+        factor = sb.tile([P, I], F32, name="factor")
 
         for h in range(2):
             nc.scalar.activation(opponent[:, halves[h]], a[:].indirect(opponent_list[:, list_halves[h]]), ACT.Copy)
@@ -125,69 +123,78 @@ def tile_attend_seconded_outside_moved_heads_kernel(
         for h in range(2):
             nc.scalar.activation(vote[:, halves[h]], margin[:, halves[h]], ACT.Tanh)
         nc.vector.tensor_reduce(out=neg_max[:], in_=own[:], axis=AXIS.X, op=ALU.max, negate=True)
-        for h in range(2):
-            nc.vector.scalar_tensor_tensor(
-                out=score[:, halves[h]], in0=vote[:, halves[h]], scalar=lam_sb[:], in1=own[:, halves[h]],
-                op0=ALU.mult, op1=ALU.add,
-            )
-        for h in range(2):
-            nc.scalar.activation(
-                prob[:, halves[h]], score[:, halves[h]], ACT.Exp, bias=neg_max[:], accum_out=half_sums[h][:]
-            )
+        old_halves = []
+        for h, tag in enumerate(("opponent_then_old", "margin_then_old")):
+            old_half = sb.tile([P, T // 2], F32, name="old%d" % h, tag=tag)
+            nc.sync.dma_start(out=old_half[:], in_=old[:, h * T // 2 : (h + 1) * T // 2])
+            old_halves.append(old_half)
 
-        def sum_runs(h):
-            nc.vector.tensor_reduce(
-                out=run_sums[:, group_halves[h]],
-                in_=prob[:, halves[h]].rearrange("p (g r) -> p g r", r=RUN),
-                axis=AXIS.X,
-                op=ALU.add,
-            )
+        pieces = [slice(0, 128), slice(128, 256), slice(256, 512)]
+        lead, rest = slice(0, 128), slice(128, 512)
 
-        def weigh(h):
+        def runs(slots):
+            return slice(slots.start // RUN, slots.stop // RUN)
+
+        def by_run(tile, slots):
+            return tile[:, slots].rearrange("p (g r) -> p g r", r=RUN)
+
+        def wide(slots):
+            count = (slots.stop - slots.start) // RUN
+            return neg_recip[:, runs(slots)].unsqueeze(2).to_broadcast([P, count, RUN])
+
+        def sum_runs(slots):
+            nc.vector.tensor_reduce(out=run_sums[:, runs(slots)], in_=by_run(prob, slots), axis=AXIS.X, op=ALU.add)
+
+        def weigh(slots):
             nc.vector.scalar_tensor_tensor(
-                out=numer[:, halves[h]], in0=prob[:, halves[h]], scalar=-64.0, in1=gain[:, halves[h]],
+                out=numer[:, slots], in0=prob[:, slots], scalar=-64.0, in1=gain[:, slots],
                 op0=ALU.mult, op1=ALU.mult,
             )
 
-        def outside(h):
+        def outside(slots):
             nc.vector.tensor_scalar(
-                out=neg_outside[:, group_halves[h]], in0=run_sums[:, group_halves[h]],
-                scalar1=half_sums[0][:], scalar2=half_sums[1][:],
+                out=neg_outside[:, runs(slots)], in0=run_sums[:, runs(slots)],
+                scalar1=front_sum[:], scalar2=piece_sums[2][:],
                 op0=ALU.subtract, op1=ALU.subtract,
             )
 
-        def invert(h):
-            nc.vector.reciprocal(out=neg_recip[:, group_halves[h]], in_=neg_outside[:, group_halves[h]])
+        def invert(slots):
+            nc.vector.reciprocal(out=neg_recip[:, runs(slots)], in_=neg_outside[:, runs(slots)])
 
-        def spread(h, copy):
-            copy(
-                out=neg_recip_wide[h][:],
-                in_=neg_recip[:, group_halves[h]].unsqueeze(2).to_broadcast([P, G // 2, RUN]),
-            )
-
-        def place(h):
+        def place(slots, values):
             nc.vector.tensor_tensor(
-                placed[:].indirect(place_list[:, list_halves[h]]),
-                numer[:, halves[h]],
-                neg_recip_wide[h][:].rearrange("p g r -> p (g r)"),
-                ALU.mult,
+                placed[:].indirect(place_list[:, slots.start // 16 : slots.stop // 16]),
+                values[:, slots], factor[:, slots], ALU.mult,
             )
 
-        sum_runs(0)
-        weigh(0)
-        outside(0)
-        sum_runs(1)
-        invert(0)
-        outside(1)
-        weigh(1)
-        spread(0, nc.vector.tensor_copy)
-        invert(1)
-        place(0)
-        spread(1, nc.scalar.copy)
-        place(1)
+        for slots in pieces:
+            nc.vector.scalar_tensor_tensor(
+                out=score[:, slots], in0=vote[:, slots], scalar=lam_sb[:], in1=own[:, slots],
+                op0=ALU.mult, op1=ALU.add,
+            )
+        for c, slots in enumerate(pieces):
+            nc.scalar.activation(prob[:, slots], score[:, slots], ACT.Exp, bias=neg_max[:], accum_out=piece_sums[c][:])
+
+        sum_runs(pieces[0])
+        nc.vector.tensor_tensor(front_sum[:], piece_sums[0][:], piece_sums[1][:], ALU.add)
+        sum_runs(pieces[1])
+        weigh(pieces[1])
+        outside(lead)
+        sum_runs(pieces[2])
+        invert(lead)
+        weigh(pieces[2])
+        outside(rest)
+        nc.vector.scalar_tensor_tensor(
+            out=by_run(factor, lead), in0=by_run(gain, lead), scalar=-64.0, in1=wide(lead), op0=ALU.mult, op1=ALU.mult
+        )
+        invert(rest)
+        place(lead, prob)
+        nc.scalar.copy(out=by_run(factor, rest), in_=wide(rest))
+        place(rest, numer)
 
         for n in range(T // OUT_TILE):
             cols = slice(n * OUT_TILE, (n + 1) * OUT_TILE)
             result = sb.tile([P, OUT_TILE], F32, name="result%d" % n)
-            nc.vector.tensor_tensor(result[:], placed[:, cols], old_sb[:, cols], ALU.add)
+            within = slice(cols.start % (T // 2), cols.start % (T // 2) + OUT_TILE)
+            nc.vector.tensor_tensor(result[:], placed[:, cols], old_halves[cols.start // (T // 2)][:, within], ALU.add)
             nc.sync.dma_start(out=out[:, cols], in_=result[:])

@@ -41,14 +41,16 @@ def tile_attend_seconded_outside_moved_heads_kernel(
 
         q_raw = sb.tile([P, PACK, Q], F32, name="q_raw", tag="query_then_gain")
         nc.sync.dma_start(out=q_raw[:], in_=query.rearrange("(p j) q -> p j q", j=PACK))
+        word_rows = keys_words[0].bitcast(I32)
+        k_words = [sb.tile([P, T], U8, name="k_words%d" % h, align_bytes=64) for h in range(2)]
+        nc.sync.dma_start(out=k_words[0][:].bitcast(I32), in_=word_rows[:, 0 : T // 4])
         scale_words = keys_scales[0].bitcast(I32)
         for quad in range(4):
             nc.sync.dma_start(
                 out=k_scales[32 * quad : 32 * quad + 4, :].bitcast(I32),
                 in_=scale_words[4 * quad : 4 * quad + 4, :],
             )
-        k_words = sb.tile([P, 2 * T], U8, name="k_words", align_bytes=64)
-        nc.sync.dma_start(out=k_words[:].bitcast(I32), in_=keys_words[0].bitcast(I32))
+        nc.sync.dma_start(out=k_words[1][:].bitcast(I32), in_=word_rows[:, T // 4 : T // 2])
 
         opponent_list = sb.tile([P, LIST_COLS], U16, name="opponent_list")
         nc.sync.dma_start(opponent_list[:], offs3)
@@ -63,7 +65,11 @@ def tile_attend_seconded_outside_moved_heads_kernel(
         nc.sync.dma_start(out=lam_sb[:], in_=lam)
 
         q_grouped = sb.tile([P, Q, PACK], BF16, name="q_grouped", align_bytes=64)
-        nc.vector.tensor_copy(out=q_grouped[:], in_=q_raw[:].rearrange("p j q -> p q j"))
+        for copy, rows in ((nc.vector.tensor_copy, slice(0, 80)), (nc.scalar.copy, slice(80, Q))):
+            copy(
+                out=q_grouped[:, rows, :].rearrange("p (c i) j -> p c j i", i=4),
+                in_=q_raw[:, :, rows].rearrange("p j (c i) -> p c j i", i=4),
+            )
         gain = sb.tile([P, I], F32, name="gain", tag="query_then_gain")
         nc.sync.dma_start(out=gain[:], in_=gainm)
         q_codes = sb.tile([P, Q], U32, name="q_codes", align_bytes=64)
@@ -79,12 +85,13 @@ def tile_attend_seconded_outside_moved_heads_kernel(
         for n, width in enumerate(PASS_WIDTHS):
             cols = slice(first, first + width)
             first = first + width
+            word_bytes = slice(2 * (cols.start % (T // 2)), 2 * (cols.start % (T // 2) + width))
             bank = ps.tile([P, width], F32, name="bank%d" % n)
             nc.tensor.matmul_mx(
                 out=bank[:],
                 lhsT=q_codes[:].bitcast(FP8X4),
                 lhsT_scale=q_scales[:],
-                rhs=k_words[:, 2 * cols.start : 2 * cols.stop].bitcast(FP4X4),
+                rhs=k_words[cols.start // (T // 2)][:, word_bytes].bitcast(FP4X4),
                 rhs_scale=k_scales[:, cols],
                 start=True,
                 stop=True,
@@ -102,15 +109,16 @@ def tile_attend_seconded_outside_moved_heads_kernel(
         margin = sb.tile([P, I], F32, name="margin", tag="margin_then_old")
         vote = sb.tile([P, I], F32, name="vote")
         score = sb.tile([P, I], F32, name="score")
-        prob = sb.tile([P, I], F32, name="prob")
+        front_prob = sb.tile([P, HALF], F32, name="front_prob")
         numer = sb.tile([P, I], F32, name="numer")
         neg_max = sb.tile([P, 1], F32, name="neg_max")
         piece_sums = [sb.tile([P, 1], F32, name="piece_sum%d" % c) for c in range(3)]
         front_sum = sb.tile([P, 1], F32, name="front_sum")
         run_sums = sb.tile([P, G], F32, name="run_sums")
         neg_outside = sb.tile([P, G], F32, name="neg_outside")
-        neg_recip = sb.tile([P, G], F32, name="neg_recip")
-        factor = sb.tile([P, I], F32, name="factor")
+        neg_recip = [sb.tile([P, G // 2], F32, name="neg_recip%d" % h) for h in range(2)]
+        factor_lead = sb.tile([P, 128], F32, name="factor_lead")
+        factor_rest = sb.tile([P, 384], F32, name="factor_rest")
 
         for h in range(2):
             nc.scalar.activation(opponent[:, halves[h]], a[:].indirect(opponent_list[:, list_halves[h]]), ACT.Copy)
@@ -140,14 +148,18 @@ def tile_attend_seconded_outside_moved_heads_kernel(
 
         def wide(slots):
             count = (slots.stop - slots.start) // RUN
-            return neg_recip[:, runs(slots)].unsqueeze(2).to_broadcast([P, count, RUN])
+            first_run = slots.start % HALF // RUN
+            return neg_recip[slots.start // HALF][:, first_run : first_run + count].unsqueeze(2).to_broadcast([P, count, RUN])
+
+        def prob_tile(slots):
+            return front_prob if slots.start < HALF else numer
 
         def sum_runs(slots):
-            nc.vector.tensor_reduce(out=run_sums[:, runs(slots)], in_=by_run(prob, slots), axis=AXIS.X, op=ALU.add)
+            nc.vector.tensor_reduce(out=run_sums[:, runs(slots)], in_=by_run(prob_tile(slots), slots), axis=AXIS.X, op=ALU.add)
 
         def weigh(slots):
             nc.vector.scalar_tensor_tensor(
-                out=numer[:, slots], in0=prob[:, slots], scalar=-64.0, in1=gain[:, slots],
+                out=numer[:, slots], in0=prob_tile(slots)[:, slots], scalar=-64.0, in1=gain[:, slots],
                 op0=ALU.mult, op1=ALU.mult,
             )
 
@@ -159,12 +171,12 @@ def tile_attend_seconded_outside_moved_heads_kernel(
             )
 
         def invert(slots):
-            nc.vector.reciprocal(out=neg_recip[:, runs(slots)], in_=neg_outside[:, runs(slots)])
+            nc.vector.reciprocal(out=neg_recip[slots.start // HALF][:], in_=neg_outside[:, runs(slots)])
 
-        def place(slots, values):
+        def place(slots, factor):
             nc.vector.tensor_tensor(
                 placed[:].indirect(place_list[:, slots.start // 16 : slots.stop // 16]),
-                values[:, slots], factor[:, slots], ALU.mult,
+                numer[:, slots], factor[:], ALU.mult,
             )
 
         for slots in pieces:
@@ -173,24 +185,23 @@ def tile_attend_seconded_outside_moved_heads_kernel(
                 op0=ALU.mult, op1=ALU.add,
             )
         for c, slots in enumerate(pieces):
-            nc.scalar.activation(prob[:, slots], score[:, slots], ACT.Exp, bias=neg_max[:], accum_out=piece_sums[c][:])
+            nc.scalar.activation(prob_tile(slots)[:, slots], score[:, slots], ACT.Exp, bias=neg_max[:], accum_out=piece_sums[c][:])
 
         sum_runs(pieces[0])
-        nc.vector.tensor_tensor(front_sum[:], piece_sums[0][:], piece_sums[1][:], ALU.add)
         sum_runs(pieces[1])
-        weigh(pieces[1])
-        outside(lead)
-        sum_runs(pieces[2])
-        invert(lead)
-        weigh(pieces[2])
-        outside(rest)
-        nc.vector.scalar_tensor_tensor(
-            out=by_run(factor, lead), in0=by_run(gain, lead), scalar=-64.0, in1=wide(lead), op0=ALU.mult, op1=ALU.mult
-        )
-        invert(rest)
-        place(lead, prob)
-        nc.scalar.copy(out=by_run(factor, rest), in_=wide(rest))
-        place(rest, numer)
+        nc.vector.tensor_tensor(front_sum[:], piece_sums[0][:], piece_sums[1][:], ALU.add)
+        weigh(halves[0])
+        outside(halves[0])
+        sum_runs(halves[1])
+        invert(halves[0])
+        outside(halves[1])
+        weigh(halves[1])
+        invert(halves[1])
+        nc.scalar.copy(out=by_run(factor_lead, lead), in_=wide(lead))
+        place(lead, factor_lead)
+        for slots in pieces[1:]:
+            nc.scalar.copy(out=by_run(factor_rest, slice(slots.start - 128, slots.stop - 128)), in_=wide(slots))
+        place(rest, factor_rest)
 
         for n in range(T // OUT_TILE):
             cols = slice(n * OUT_TILE, (n + 1) * OUT_TILE)

@@ -21,7 +21,7 @@ PACK = 4
 PASS_WIDTHS = (256, 256, 256, 128, 128)
 HALF = I // 2
 LIST_COLS = I // 16
-OUT_TILE = 256
+STORE_WIDTHS = (256, 256, 256, 128, 128)
 
 FLOPS = 2 * D * Q * T
 
@@ -120,10 +120,9 @@ def tile_attend_seconded_outside_moved_heads_kernel(
         factor_lead = sb.tile([P, 128], F32, name="factor_lead")
         factor_rest = sb.tile([P, 384], F32, name="factor_rest")
 
-        for h in range(2):
-            nc.scalar.activation(opponent[:, halves[h]], a[:].indirect(opponent_list[:, list_halves[h]]), ACT.Copy)
-        nc.vector.tensor_copy(own[:, halves[0]], a[:].indirect(own_list[:, list_halves[0]]))
-        nc.scalar.activation(own[:, halves[1]], a[:].indirect(own_list[:, list_halves[1]]), ACT.Copy)
+        nc.vector.tensor_copy(opponent[:, halves[0]], a[:].indirect(opponent_list[:, list_halves[0]]))
+        nc.scalar.activation(opponent[:, halves[1]], a[:].indirect(opponent_list[:, list_halves[1]]), ACT.Copy)
+        nc.scalar.activation(own[:], a[:].indirect(own_list[:]), ACT.Copy)
         for h in range(2):
             nc.vector.tensor_tensor(
                 margin[:, halves[h]], a[:].indirect(seconder_list[:, list_halves[h]]), opponent[:, halves[h]], ALU.subtract
@@ -203,9 +202,11 @@ def tile_attend_seconded_outside_moved_heads_kernel(
             nc.scalar.copy(out=by_run(factor_rest, slice(slots.start - 128, slots.stop - 128)), in_=wide(slots))
         place(rest, factor_rest)
 
-        for n in range(T // OUT_TILE):
-            cols = slice(n * OUT_TILE, (n + 1) * OUT_TILE)
-            result = sb.tile([P, OUT_TILE], F32, name="result%d" % n)
-            within = slice(cols.start % (T // 2), cols.start % (T // 2) + OUT_TILE)
+        first = 0
+        for n, width in enumerate(STORE_WIDTHS):
+            cols = slice(first, first + width)
+            first = first + width
+            result = sb.tile([P, width], F32, name="result%d" % n)
+            within = slice(cols.start % (T // 2), cols.start % (T // 2) + width)
             nc.vector.tensor_tensor(result[:], placed[:, cols], old_halves[cols.start // (T // 2)][:, within], ALU.add)
             nc.sync.dma_start(out=out[:, cols], in_=result[:])

from contextlib import ExitStack

import concourse.mybir as mybir

F32 = mybir.dt.float32
BF16 = mybir.dt.bfloat16
I32 = mybir.dt.int32
U32 = mybir.dt.uint32
U16 = mybir.dt.uint16
U8 = mybir.dt.uint8
FP8X4 = mybir.dt.float8_e4m3fn_x4
FP4X4 = mybir.dt.float4_e2m1fn_x4
ALU = mybir.AluOpType
ACT = mybir.ActivationFunctionType
AXIS = mybir.AxisListType

P = 128
D, T, I, Q, G = 512, 1024, 512, 128, 64
RUN = I // G
PACK = 4
PASS_WIDTHS = (256, 256, 256, 128, 128)
HALF = I // 2
LIST_COLS = I // 16
STORE_WIDTHS = (256, 256, 256, 128, 128)

FLOPS = 2 * D * Q * T


def tile_attend_seconded_outside_moved_heads_kernel(
    tc, query, keys_words, keys_scales, lam, old, gainm, offs, offs2, offs3, offs4, out
):
    nc = tc.nc
    with ExitStack() as ctx:
        sb = ctx.enter_context(tc.tile_pool(name="sb", bufs=1))
        ps = ctx.enter_context(tc.psum_pool(name="ps", bufs=1))

        k_scales = sb.tile([P, T], U8, name="k_scales", align_bytes=64)
        nc.vector.memset(k_scales[:].bitcast(I32), 0)
        placed = sb.tile([P, T], F32, name="placed")
        nc.vector.memset(placed[:], 0.0)

        q_raw = sb.tile([P, PACK, Q], F32, name="q_raw", tag="query_then_gain")
        nc.sync.dma_start(out=q_raw[:], in_=query.rearrange("(p j) q -> p j q", j=PACK))
        word_rows = keys_words[0].bitcast(I32)
        k_words = [sb.tile([P, T], U8, name="k_words%d" % h, align_bytes=64) for h in range(2)]
        nc.sync.dma_start(out=k_words[0][:].bitcast(I32), in_=word_rows[:, 0 : T // 4])
        scale_words = keys_scales[0].bitcast(I32)
        for quad in range(4):
            nc.sync.dma_start(
                out=k_scales[32 * quad : 32 * quad + 4, :].bitcast(I32),
                in_=scale_words[4 * quad : 4 * quad + 4, :],
            )
        nc.sync.dma_start(out=k_words[1][:].bitcast(I32), in_=word_rows[:, T // 4 : T // 2])

        opponent_list = sb.tile([P, LIST_COLS], U16, name="opponent_list")
        nc.sync.dma_start(opponent_list[:], offs3)
        own_list = sb.tile([P, LIST_COLS], U16, name="own_list")
        nc.sync.dma_start(own_list[:], offs)
        seconder_list = sb.tile([P, LIST_COLS], U16, name="seconder_list")
        nc.sync.dma_start(seconder_list[:], offs2)
        place_list = sb.tile([P, LIST_COLS], U16, name="place_list")
        nc.sync.dma_start(place_list[:], offs4)

        lam_sb = sb.tile([P, 1], F32, name="lam_sb")
        nc.sync.dma_start(out=lam_sb[:], in_=lam)

        q_grouped = sb.tile([P, Q, PACK], BF16, name="q_grouped", align_bytes=64)
        for copy, rows in ((nc.vector.tensor_copy, slice(0, 80)), (nc.scalar.copy, slice(80, Q))):
            copy(
                out=q_grouped[:, rows, :].rearrange("p (c i) j -> p c j i", i=4),
                in_=q_raw[:, :, rows].rearrange("p j (c i) -> p c j i", i=4),
            )
        gain = sb.tile([P, I], F32, name="gain", tag="query_then_gain")
        nc.sync.dma_start(out=gain[:], in_=gainm)
        q_codes = sb.tile([P, Q], U32, name="q_codes", align_bytes=64)
        q_scales = sb.tile([P, Q], U8, name="q_scales", align_bytes=64)
        nc.vector.quantize_mx(
            out=q_codes[:].bitcast(FP8X4),
            scales=q_scales[:],
            in_=q_grouped[:].rearrange("p q j -> p (q j)"),
        )

        a = sb.tile([P, T], F32, name="a")
        first = 0
        for n, width in enumerate(PASS_WIDTHS):
            cols = slice(first, first + width)
            first = first + width
            word_bytes = slice(2 * (cols.start % (T // 2)), 2 * (cols.start % (T // 2) + width))
            bank = ps.tile([P, width], F32, name="bank%d" % n)
            nc.tensor.matmul_mx(
                out=bank[:],
                lhsT=q_codes[:].bitcast(FP8X4),
                lhsT_scale=q_scales[:],
                rhs=k_words[cols.start // (T // 2)][:, word_bytes].bitcast(FP4X4),
                rhs_scale=k_scales[:, cols],
                start=True,
                stop=True,
            )
            if n % 2 == 1:
                nc.scalar.copy(out=a[:, cols], in_=bank[:])
            else:
                nc.vector.tensor_copy(out=a[:, cols], in_=bank[:])

        halves = [slice(h * HALF, (h + 1) * HALF) for h in range(2)]
        list_halves = [slice(h * LIST_COLS // 2, (h + 1) * LIST_COLS // 2) for h in range(2)]

        opponent = sb.tile([P, I], F32, name="opponent", tag="opponent_then_old")
        own = sb.tile([P, I], F32, name="own")
        margin = sb.tile([P, I], F32, name="margin", tag="margin_then_old")
        vote = sb.tile([P, I], F32, name="vote")
        score = sb.tile([P, I], F32, name="score")
        front_prob = sb.tile([P, HALF], F32, name="front_prob")
        numer = sb.tile([P, I], F32, name="numer")
        neg_max = sb.tile([P, 1], F32, name="neg_max")
        piece_sums = [sb.tile([P, 1], F32, name="piece_sum%d" % c) for c in range(3)]
        front_sum = sb.tile([P, 1], F32, name="front_sum")
        run_sums = sb.tile([P, G], F32, name="run_sums")
        neg_outside = sb.tile([P, G], F32, name="neg_outside")
        neg_recip = [sb.tile([P, G // 2], F32, name="neg_recip%d" % h) for h in range(2)]
        factor_lead = sb.tile([P, 128], F32, name="factor_lead")
        factor_rest = sb.tile([P, 384], F32, name="factor_rest")

        nc.vector.tensor_copy(opponent[:, halves[0]], a[:].indirect(opponent_list[:, list_halves[0]]))
        nc.scalar.activation(opponent[:, halves[1]], a[:].indirect(opponent_list[:, list_halves[1]]), ACT.Copy)
        nc.scalar.activation(own[:], a[:].indirect(own_list[:]), ACT.Copy)
        for h in range(2):
            nc.vector.tensor_tensor(
                margin[:, halves[h]], a[:].indirect(seconder_list[:, list_halves[h]]), opponent[:, halves[h]], ALU.subtract
            )
        for h in range(2):
            nc.scalar.activation(vote[:, halves[h]], margin[:, halves[h]], ACT.Tanh)
        nc.vector.tensor_reduce(out=neg_max[:], in_=own[:], axis=AXIS.X, op=ALU.max, negate=True)
        old_halves = []
        for h, tag in enumerate(("opponent_then_old", "margin_then_old")):
            old_half = sb.tile([P, T // 2], F32, name="old%d" % h, tag=tag)
            nc.sync.dma_start(out=old_half[:], in_=old[:, h * T // 2 : (h + 1) * T // 2])
            old_halves.append(old_half)

        pieces = [slice(0, 128), slice(128, 256), slice(256, 512)]
        lead, rest = slice(0, 128), slice(128, 512)

        def runs(slots):
            return slice(slots.start // RUN, slots.stop // RUN)

        def by_run(tile, slots):
            return tile[:, slots].rearrange("p (g r) -> p g r", r=RUN)

        def wide(slots):
            count = (slots.stop - slots.start) // RUN
            first_run = slots.start % HALF // RUN
            return neg_recip[slots.start // HALF][:, first_run : first_run + count].unsqueeze(2).to_broadcast([P, count, RUN])

        def prob_tile(slots):
            return front_prob if slots.start < HALF else numer

        def sum_runs(slots):
            nc.vector.tensor_reduce(out=run_sums[:, runs(slots)], in_=by_run(prob_tile(slots), slots), axis=AXIS.X, op=ALU.add)

        def weigh(slots):
            nc.vector.scalar_tensor_tensor(
                out=numer[:, slots], in0=prob_tile(slots)[:, slots], scalar=-64.0, in1=gain[:, slots],
                op0=ALU.mult, op1=ALU.mult,
            )

        def outside(slots):
            nc.vector.tensor_scalar(
                out=neg_outside[:, runs(slots)], in0=run_sums[:, runs(slots)],
                scalar1=front_sum[:], scalar2=piece_sums[2][:],
                op0=ALU.subtract, op1=ALU.subtract,
            )

        def invert(slots):
            nc.vector.reciprocal(out=neg_recip[slots.start // HALF][:], in_=neg_outside[:, runs(slots)])

        def place(slots, factor):
            nc.vector.tensor_tensor(
                placed[:].indirect(place_list[:, slots.start // 16 : slots.stop // 16]),
                numer[:, slots], factor[:], ALU.mult,
            )

        for slots in pieces:
            nc.vector.scalar_tensor_tensor(
                out=score[:, slots], in0=vote[:, slots], scalar=lam_sb[:], in1=own[:, slots],
                op0=ALU.mult, op1=ALU.add,
            )
        for c, slots in enumerate(pieces):
            nc.scalar.activation(prob_tile(slots)[:, slots], score[:, slots], ACT.Exp, bias=neg_max[:], accum_out=piece_sums[c][:])

        sum_runs(pieces[0])
        sum_runs(pieces[1])
        nc.vector.tensor_tensor(front_sum[:], piece_sums[0][:], piece_sums[1][:], ALU.add)
        weigh(halves[0])
        outside(halves[0])
        sum_runs(halves[1])
        invert(halves[0])
        outside(halves[1])
        weigh(halves[1])
        invert(halves[1])
        nc.scalar.copy(out=by_run(factor_lead, lead), in_=wide(lead))
        place(lead, factor_lead)
        for slots in pieces[1:]:
            nc.scalar.copy(out=by_run(factor_rest, slice(slots.start - 128, slots.stop - 128)), in_=wide(slots))
        place(rest, factor_rest)

        first = 0
        for n, width in enumerate(STORE_WIDTHS):
            cols = slice(first, first + width)
            first = first + width
            result = sb.tile([P, width], F32, name="result%d" % n)
            within = slice(cols.start % (T // 2), cols.start % (T // 2) + width)
            nc.vector.tensor_tensor(result[:], placed[:, cols], old_halves[cols.start // (T // 2)][:, within], ALU.add)
            nc.sync.dma_start(out=out[:, cols], in_=result[:])
